import numpy as np, ml_dtypes
CORES = [16,17,18,19,32,33,34,35]
N = 8
BF = ml_dtypes.bfloat16
V, C, S, IT, Q, RO, D = 2560, 256, 128, 3, 6, 2, 2048
P = V + 2 * C * RO
def mesh(rng, m, isb, chain):
    o = rng.permutation(V); x = np.zeros(3 * V, np.int64); sn = np.zeros(2 * S, np.int64); rest = V - 2 * m
    x[2 * V + o[0:2 * m:2]] = o[1:2 * m:2]; x[2 * V + o[1:2 * m:2]] = o[0:2 * m:2]
    up = 2 * V + o[2 * m:]; leg = rng.integers(0, 2, rest) * V + o[:rest] if chain else rng.permutation(2 * V)[:rest]
    left = np.ones(2 * V, bool); left[leg] = False
    jb, jl = np.flatnonzero(isb), np.flatnonzero(~isb); c = rng.permutation(rest); cut, keep = c[:len(jb)], c[len(jb):]
    x[up[keep]] = leg[keep] % V; x[leg[keep]] = up[keep] - 2 * V
    x[up[cut]] = P + jb; sn[jb] = up[cut] - 2 * V
    pool = np.concatenate([rng.permutation(leg[cut]), rng.permutation(np.flatnonzero(left))]); h = rng.permutation(pool[:len(jl)])
    x[h] = P + jl; sn[jl] = h % V
    k = rng.permutation(pool[len(jl):]).reshape(2, -1); x[k[0]] = k[1] % V; x[k[1]] = k[0] % V
    return x.reshape(3, V), sn, o
def meshes(rng, m, chain=False):
    x = rng.choice(4, (N, 8, S), p=[0.35, 0.35, 0.2, 0.1])
    isb = np.concatenate([np.roll((x == 1) | (x == 3), 1, axis=0), (x == 0) | (x == 3)], axis=2)
    z = [[mesh(rng, int(m[a, g]), isb[a, g], chain) for g in range(8)] for a in range(N)]
    return tuple(np.stack([np.stack([u[i] for u in row]) for row in z]) for i in range(3))
def levels(rng):
    return rng.permuted(np.tile(np.array([60, 90, 110, 130, 150, 165, 180, 200]), (N, 1)), axis=1)[:, :, None, None] + rng.integers(-20, 21, (N, 8, 16, 1))
def errors(rng):
    return (256 * (0.25 + 0.75 * rng.random((N, 8, 1, V))) * rng.random((N, 8, 16, V))).astype(np.int64)
def under(rng, th):
    return np.minimum((th * rng.random((N, 8, 16, V))).astype(np.int64), th - 1)
def plant(rng, e, t, x, y, cnt):
    on = np.argsort(rng.random((16, len(x))), axis=0) < cnt[None, :]; one = rng.random(on.shape) < 0.5
    v = np.where(rng.random(on.shape) < 0.5, t, np.minimum(t + (rng.random(on.shape) * (256 - t)).astype(np.int64), 255))
    e[:, x] = np.where(on & one, v, e[:, x]); e[:, y] = np.where(on & ~one, v, e[:, y])
def more(rng):
    return rng.integers(0, 256, (N, 8, 16, D)), rng.integers(0, 256, (N, 8, 16, 1))
def pack(err, p, sn, det, wt, th):
    b = lambda a: np.ascontiguousarray(a.reshape(N, 128, -1)).astype(np.float32).astype(BF)
    i = lambda a: np.ascontiguousarray(a).astype(np.int32)
    return {"err": b(err), "lt": i(p[:, :, 0]), "rt": i(p[:, :, 1]), "bs": i(p[:, :, 2]), "snd": i(sn), "det": b(det), "wt": i(wt.reshape(N, 128, 1)), "th": i(th.reshape(N, 128, 1))}
def setup_inputs(rng):
    p, sn, o = meshes(rng, rng.integers(V // 8, V // 3 + 1, (N, 8))); det, wt = more(rng)
    return pack(errors(rng), p, sn, det, wt, levels(rng))
def setup_inputs_room(rng):
    M = V // 3; p, sn, o = meshes(rng, np.full((N, 8), M)); det, wt = more(rng)
    th = np.repeat(rng.integers(64, 192, (1, 8, 16, 1)), N, axis=0); err = under(rng, th)
    for a in range(N):
        for g in range(8):
            n = (C, C + 1, 0, 1, C - 1, M, C, C + 1)[(a + g) % 8]
            plant(rng, err[a, g], th[a, g], o[a, g, 0:2 * M:2], o[a, g, 1:2 * M:2], np.where(rng.permutation(M) < n, Q, Q - 1))
    return pack(err, p, sn, det, wt, th)
def setup_inputs_chain(rng):
    M = V // (2 * (IT + 3)); p, sn, o = meshes(rng, np.full((N, 8), M), True); det, wt = more(rng)
    th = np.repeat(rng.integers(64, 192, (1, 8, 16, 1)), N, axis=0); err = under(rng, th); far = np.array([0, 1, IT - 1, IT, IT, IT + 1, IT + 1])
    for a in range(N):
        for g in range(8):
            i = 2 * np.arange(M) + 2 * M * rng.permuted(np.resize(far, M))
            plant(rng, err[a, g], th[a, g], o[a, g, i], o[a, g, i + 1], np.where(rng.random(M) < 0.8, Q, Q - 1))
    return pack(err, p, sn, det, wt, th)
def setup_inputs_ties(rng):
    p, sn, o = meshes(rng, rng.integers(V // 8, V // 3 + 1, (N, 8))); det, wt = more(rng)
    th = np.clip(np.array([1, 2, 100, 128, 254, 255, 255, 30])[None, :, None, None] + rng.integers(-1, 2, (N, 8, 16, 1)), 1, 255); th[:, 6] = 255
    err = np.clip(th - 1 + (rng.random((N, 8, 16, V)) < 0.5 * rng.random((N, 8, 1, V))) * rng.integers(1, 3, (N, 8, 16, V)), 0, 255)
    err[:, 6] = np.minimum(err[:, 6], 254); err[:, 7] = 255
    det[:, 1] = 255; det[:, 2] = 0; wt[:, 0] = 0; wt[:, 1] = 255
    return pack(err, p, sn, det, wt, th)
def pools(rng):
    return [[int(z) for z in rng.permutation(V)] for a in range(N)], rng.permutation(S)[:8 * N].reshape(N, 2, 4)
def watch(x, leg, u, v, slot):
    x[leg, u] = P + slot; x[1 - leg, u] = v; x[2, u] = v; x[:, v] = u
def renamed(rng, x, sn, e):
    pool, kk = pools(rng)
    for a in range(N):
        for s in range(2):
            k, k2, kb, kb2 = [int(z) for z in kk[a, s]]; q, z = (a + 2 * s - 1) % N, (a - 2 * s + 1) % N
            t, b = pool[a].pop(), pool[a].pop()
            x[a, 2, t] = b; x[a, 2, b] = t; x[a, 0, t] = P + (1 - s) * S + k2; x[a, 1, t] = P + s * S + k; e[a, :, t] = 255
            sn[a, s * S + k] = t; sn[a, (1 - s) * S + k] = t
            u, v = pool[q].pop(), pool[q].pop(); sn[q, (1 - s) * S + k] = u; watch(x[q], s, u, v, (1 - s) * S + k)
            u, v = pool[z].pop(), pool[z].pop(); sn[z, s * S + k2] = u; watch(x[z], 1 - s, u, v, s * S + k)
            t, b = pool[a].pop(), pool[a].pop()
            x[a, 2, t] = b; x[a, 2, b] = t; x[a, 0, t] = P + s * S + kb2; e[a, :, t] = 255
            x[a, 1, t] = (P + s * S + kb) % (2 * S) + 2 * S * int(rng.integers(0, V // (2 * S))); sn[a, s * S + kb] = t
            u, v = pool[q].pop(), pool[q].pop(); sn[q, (1 - s) * S + kb2] = u; watch(x[q], s, u, v, (1 - s) * S + kb)
def allpairs(rng, x, e):
    for a in range(N):
        pr = np.sort(rng.permutation(V).reshape(-1, 2), axis=1); pr = pr[np.argsort(pr[:, 0])]
        x[a, 0, pr[0::2]] = pr[1::2]; x[a, 0, pr[1::2]] = pr[0::2]
        for i in (1, 2):
            x[a, i, pr[:, 0]] = pr[:, 1]; x[a, i, pr[:, 1]] = pr[:, 0]
        e[a][:, pr[len(pr) - C // 2:].reshape(-1)] = 255
def crowded(rng, x, sn, e):
    pool, kk = pools(rng)
    for a in range(N):
        for s in range(2):
            q = (a + 2 * s - 1) % N
            for i in range(2):
                k, kn = int(kk[a, s, 2 * i]), int(kk[a, s, 2 * i + 1]); many = [pool[a].pop() for z in range(V // 16)]
                x[a, 2, np.array(many)] = P + s * S + kn
                t = max(many) if i == 0 else min(many); e[a, :, t] = 255; sn[a, s * S + k] = t
                u, v = pool[q].pop(), pool[q].pop(); sn[q, (1 - s) * S + kn] = u; watch(x[q], 1 - i, u, v, (1 - s) * S + k)
def newbases(rng, x, sn, e, th):
    pool, kk = pools(rng)
    for a in range(N):
        pr = np.sort(np.array(pool[a][:2 * S]).reshape(S, 2), axis=1); pr = pr[np.argsort(pr[:, 0])]
        x[a, 2, pr[:, 0]] = pr[:, 1]; x[a, 2, pr[:, 1]] = pr[:, 0]
        plant(rng, e[a], th[a], pr[:, 0], pr[:, 1], rng.integers(Q, 17, S))
        for s in range(2):
            q = (a + 2 * s - 1) % N
            for i in range(2):
                k, kn = int(kk[a, s, 2 * i]), int(kk[a, s, 2 * i + 1]); j = (s * S + kn + P - V) % (2 * S)
                y = int(pr[j // 2, j % 2]); w = pool[a].pop()
                x[a, :, w] = y; x[a, 1, y] = w; e[a, :, w] = 255; sn[a, s * S + k] = w
                u, v = pool[q].pop(), pool[q].pop(); sn[q, (1 - s) * S + kn] = u; watch(x[q], i, u, v, (1 - s) * S + k)
def setup_inputs_free(rng):
    p = rng.choice(np.concatenate([np.arange(V), P + np.arange(2 * S)]), (N, 8, 3, V)); sn = rng.integers(0, V, (N, 8, 2 * S)); m = V // 4
    det, wt = more(rng); err = errors(rng); th = levels(rng)
    for a in range(N):
        for g in range(0, 8, 2):
            o = rng.permutation(V); x = p[a, g]; x[2, o[0:2 * m:2]] = o[1:2 * m:2]; x[2, o[1:2 * m:2]] = o[0:2 * m:2]
            v = o[2 * m:]; v = v[x[2, v] < V]; x[rng.integers(0, 2, len(v)), x[2, v]] = v
            x[0, o[:40]] = o[:40]; x[1, o[20:60]] = o[20:60]; x[0, o[100:140]] = x[1, o[100:140]]; x[1, o[200:240:2]] = o[201:240:2]
            j = rng.permutation(2 * S)[:S // 2]; x[1, sn[a, g, j]] = P + j
    for a in range(N):
        for g in range(0, 8, 2):
            for s in range(2):
                q = (a + 2 * s - 1) % N; k = rng.integers(0, S, 32); k2 = rng.integers(0, S, 32)
                p[q, g, 2, sn[q, g, (1 - s) * S + k]] = P + (1 - s) * S + k2
                p[a, g, rng.integers(0, 2, 32), sn[a, g, s * S + k2]] = P + s * S + k
    p[:, 0, 2, 0] = V - 1; p[:, 0, 2, V - 1] = 0; err[:, 0, :, 0] = 255; err[:, 0, :, V - 1] = 255
    n = 16; me = np.arange(V); two, lone = {}, {}
    for a in range(N):
        for g in range(0, 8, 2):
            x = p[a, g]
            b = np.minimum(x[2], V - 1); pair = (x[2] < V) & (x[2, b] == me) & (b != me)
            t = rng.permutation(np.flatnonzero(pair & (me < b) & (me > 0)))
            two[a, g] = rng.permuted(np.stack([t[:2 * n], b[t[:2 * n]]]), axis=0)
            lone[a, g] = rng.permutation(np.flatnonzero(~pair & (me > 0) & (me < V - 1)))[:2 * n]
            cut = t[C - 4 * n:]; x[2, cut] = P + rng.integers(0, 2 * S, len(cut))
    for g in range(0, 8, 2):
        k, k2 = rng.permutation(S)[:2 * n].reshape(2, n)
        for a in range(N):
            for s in range(2):
                q = (a + 2 * s - 1) % N; u, v = two[a, g][:, s * n:(s + 1) * n]; w = lone[q, g][(1 - s) * n:(2 - s) * n]
                sn[a, g, s * S + k2] = u; sn[q, g, (1 - s) * S + k] = w
                x = p[a, g]; x[0, u] = P + s * S + k; x[1, u] = v; x[0, v] = u; x[1, v] = u
                p[q, g, 2, w] = np.where(np.arange(n) < n // 2, P + s * S + k2, (P + k2) % S + S * rng.integers(0, V // S, n))
                e = err[a, g]; c = np.concatenate([u, v]); e[:, c] = np.minimum(e[:, c], th[a, g] - 1)
                plant(rng, err[q, g], th[a, g], w, w, rng.integers(Q, 17, n))
    th[:, 1::2] = rng.integers(20, 121, (N, 4, 16, 1)); err[:, 1::2] = under(rng, th)[:, 1::2]
    p[:, 1::2, 2] = P + rng.integers(0, 2 * S, (N, 4, V)); p[:, 5] = P + rng.integers(0, 2 * S, (N, 3, V))
    sn[:, 5] = rng.choice(np.array([0, V - 1, V // 2, 5]), (N, 2 * S))
    renamed(rng, p[:, 1], sn[:, 1], err[:, 1]); allpairs(rng, p[:, 3], err[:, 3])
    crowded(rng, p[:, 5], sn[:, 5], err[:, 5]); newbases(rng, p[:, 7], sn[:, 7], err[:, 7], th[:, 7])
    return pack(err, p, sn, det, wt, th)
def setup_inputs_spread(rng):
    p, sn, o = meshes(rng, rng.integers(V // 8, V // 3 + 1, (N, 8)))
    err = (np.exp2(8 * rng.random((N, 8, 1, V))) * rng.random((N, 8, 16, V))).astype(np.int64)
    det = (np.exp2(8 * rng.random((N, 8, 1, D))) * rng.random((N, 8, 16, D))).astype(np.int64)
    wt = np.minimum(np.exp2(8 * rng.random((N, 8, 16, 1))).astype(np.int64), 255)
    th = np.clip(np.exp2(3 + 5 * rng.random((N, 8, 1, 1)) + rng.random((N, 8, 16, 1)) - 0.5).astype(np.int64), 1, 255)
    return pack(np.minimum(err, 255), p, sn, np.minimum(det, 255), wt, th)
def check_inputs(d):
    bad = []
    for k in ("err", "det"):
        x = np.asarray(d[k]).astype(np.float32)
        if not np.all((x >= 0) & (x <= 255) & (x == np.floor(x))): bad.append("range of " + k)
    for k in ("lt", "rt", "bs"):
        x = d[k]
        if not np.all(((x >= 0) & (x < V)) | ((x >= P) & (x < P + 2 * S))): bad.append("range of " + k)
    for k, lo, hi in (("snd", 0, V - 1), ("wt", 0, 255), ("th", 1, 255)):
        if np.min(d[k]) < lo or np.max(d[k]) > hi: bad.append("range of " + k)
    return bad
def ghosts(x):
    return np.concatenate([np.roll(x[..., S:], 1, axis=0), np.roll(x[..., :S], -1, axis=0)], axis=-1)
def reference(err, lt, rt, bs, snd, det, wt, th):
    take = np.take_along_axis; me = np.arange(P)
    e = np.zeros((N, 8, 16, P), np.int32); e[..., :V] = err.astype(np.float32).astype(np.int32).reshape(N, 8, 16, V)
    dt = det.astype(np.float32).astype(np.int32).reshape(N, 8, 16, D); wq = wt.astype(np.int32).reshape(N, 8, 16, 1); tq = th.astype(np.int32).reshape(N, 8, 16, 1)
    p = np.zeros((N, 8, 3, P), np.int64) + me
    p[:, :, 0, :V] = lt; p[:, :, 1, :V] = rt; p[:, :, 2, :V] = bs
    sn = snd.astype(np.int64)
    lo = np.repeat(np.array([0, S]), S); off = np.repeat(np.array([-S, S]), S)
    for t in range(RO):
        L, R, B = p[:, :, 0], p[:, :, 1], p[:, :, 2]
        j = ghosts(take(B, sn, 2)) - P + off
        gb = np.where((j >= lo) & (j < lo + S), take(sn, np.clip(j, 0, 2 * S - 1), 2), -1)
        base = np.concatenate([B, gb], axis=2); gl = (take(base, L, 2) == me)[:, :, None]; gr = (take(base, R, 2) == me)[:, :, None]
        W = e
        for it in range(IT):
            A = np.concatenate([W, ghosts(take(W, sn[:, :, None], 3))], axis=3)
            W = np.maximum(W, np.maximum(np.where(gl, take(A, L[:, :, None], 3), 0), np.where(gr, take(A, R[:, :, None], 3), 0)))
        bo = np.minimum(B, P - 1); pair = (B < P) & (take(B, bo, 2) == me) & (me < B)
        rows = np.add.reduce((np.maximum(W, take(W, bo[:, :, None], 3)) >= tq).astype(np.int32), axis=2)
        go = (pair & (rows >= Q)).astype(np.int64); k = np.add.accumulate(go, axis=2) - go
        a, g, x = np.nonzero((go == 1) & (k < C)); y = B[a, g, x]
        new = np.zeros((N, 8, P), np.int64)
        new[a, g, x] = V + 2 * C * t + 2 * k[a, g, x]; new[a, g, y] = new[a, g, x] + 1
        nx = np.concatenate([new, np.zeros((N, 8, 2 * S), np.int64)], axis=2); rx = np.concatenate([R, np.full((N, 8, 2 * S), -1)], axis=2)
        pn = np.stack([np.where((take(nx, T, 2) > 0) & (take(rx, T, 2) == me), take(nx, T, 2), T) for T in (L, R, B)], axis=2)
        sn = np.where((take(new, sn, 2) > 0) & (take(R, sn, 2) == P + np.arange(2 * S)), take(new, sn, 2), sn)
        a = np.concatenate([a, a]); g = np.concatenate([g, g]); s = np.concatenate([x, y]); o = np.concatenate([y, x])
        n, m = new[a, g, s], new[a, g, o]; bl, br = pn[a, g, 0, s], pn[a, g, 1, s]
        pn[a, g, 0, s] = n; pn[a, g, 1, s] = m; pn[a, g, 2, s] = bl
        pn[a, g, 0, n] = o; pn[a, g, 1, n] = s; pn[a, g, 2, n] = br
        p = pn
        es = e[a, g, :, s]; h = np.add.reduce(wq * e, axis=2)[a, g, s]
        for place in (s, n):
            e[a, g, :, place] = (es >> 1) + (dt[a, g, :, (h + place) & (D - 1)] >> 1)
    return {"ye": e.reshape(N, 128, P).astype(np.float32).astype(BF), "yl": p[:, :, 0].astype(np.float32), "yr": p[:, :, 1].astype(np.float32), "yb": p[:, :, 2].astype(np.float32)}

import numpy as np
from concourse.bass import DstId, RemoteDMATransfer
from concourse.mybir import AluOpType as A, ActivationFunctionType as F

NR, P0, GH = 8, 2560, 3584
CP = F.Copy
W0 = 272
BIG = 16384.0
_bf = {"hi": 672, "lo": 672, "shi": 16, "slo": 16, "ihi": 224, "ilo": 224, "chi": 224, "clo": 224,
       "ev": 4112, "eu": 3856, "wa": 3344, "wb": 3344, "tb": 3840, "tc": 3840, "nt0": 3840, "nt1": 3840,
       "gl": 3072, "gr": 3072, "gb": 3072, "hb": 3072, "ec": 3072, "cv": 3072, "vf": 3072, "ct": 3328, "snf": 272,
       "zz": 2048, "zb": 2048, "zr": 2048, "zi": 2048, "zl": 2048, "zh": 2048, "bo": 128, "ltm": 128, "dr": 2048, "dh": 2064,
       "gh1": 256, "gl1": 256, "gi": 256, "zero": 192, "gs": 256, "gsb": 256, "gx": 512, "gt": 256, "gq": 512, "gy": 512, "gn": 512, "gsn": 256,
       "rl": 192, "rr": 192, "rb": 192, "eq": 192, "hot": 192, "cum": 192, "sel": 192, "n0": 192, "n1": 192, "nchi": 192, "nclo": 192, "sc": 192,
       "eg": 512, "dg": 1024, "cl": 512, "cr": 512, "x0": 256, "x1": 256, "x2": 256}
_f32 = {"px": 672, "sn": 16, "df": 2048, "ci": 8, "i8": 8, "mk2": 8, "mk": 16, "i16": 16, "cc": 224, "me": 224, "ix": 224, "ixm": 192,
        "xs": 16, "gv": 256, "bes": 16, "bel0": 16, "bel1": 16, "gm": 16, "gd": 16, "gm1": 8, "srf": 16, "sw": 16, "xv": 32, "xf": 32,
        "vl": 192, "lf": 192, "vr": 192, "rf": 192, "bf": 192, "pt": 192, "thr": 192, "k1": 192, "nt": 192, "kn": 192, "dd": 192, "nc": 192,
        "st": 192, "spl": 192, "no": 192, "nb": 192, "m8": 192, "wq": 192, "wr": 192, "fl": 32, "fo": 32, "tv": 32, "pv": 32, "rq": 32,
        "rn": 32, "nw": 96, "dq": 64, "scf": 32}
_i32 = {"xin": 480, "sin": 16, "win": 2, "pid": 4, "di": 64, "da": 64, "e2": 512}
_u16 = {"lv": 192, "rv": 192, "bv": 192, "lw": 192, "rw": 192, "bw": 192, "snu": 16, "slu": 32, "siu": 16, "gbu": 16, "xlu": 32,
        "tu16": 16, "tu": 32, "yu": 32, "du": 64, "scu": 32, "pd": 192}
SCRATCH, AL, _o = {}, {}, 0
for _k in list(_f32):
    if _f32[_k] <= 192 and _k not in ("i16", "xs", "bes", "bel0", "bel1"):
        AL[_k] = (_o, _f32[_k])
        _o += (_f32.pop(_k) + 3) // 4 * 4
_f32["pf"] = _o
for _s, _d in ((_bf, "bfloat16"), (_f32, "float32"), (_i32, "int32"), (_u16, "uint16")):
    for _k in _s:
        SCRATCH[_k] = ("sbuf", [128, _s[_k]], _d)
for _k in range(8):
    SCRATCH["ps%d" % _k] = ("psum", [128, 512], "float32")
_KINDS = ["be", "x0", "x1", "x2"]
NDMA = 110
SEMAPHORES = ["qv", "qs", "qt", "qg"] + ["a%s%d" % (k, t) for k in _KINDS for t in range(2)] + \
             ["l%s%d" % (k, t) for k in _KINDS for t in range(2)] + ["d%d" % k for k in range(NDMA)]


def tracker(g, T):
    Q = {"v": g.vector, "s": g.scalar, "t": g.tensor, "g": g, "y": g.sync}
    acc, known, snap, cnt, top = {}, {q: {} for q in Q}, {}, {q: 0 for q in Q}, {}
    nd = [0]

    def hit(x, y):
        if x[1] >= y[2] or y[1] >= x[2]:
            return False
        if x[3] > 1 and x[3] == y[3] and (x[1] - y[1]) % x[3]:
            return False
        return x[4] is None or y[4] is None or x[4] == y[4]

    def wait(q, sem, val):
        if known[q].get(sem, 0) >= val:
            return
        Q[q].wait_ge(T.sem[sem], val)
        for s, v in snap.get((sem, val), {}).items():
            if known[q].get(s, 0) < v:
                known[q][s] = v
        known[q][sem] = val

    def deps(q, reads, writes, asyn):
        need = {}
        for wr, refs in ((False, reads), (True, writes)):
            for r in refs:
                ps = r[0][:2] == "ps"
                for (x, k, tok) in acc.get(r[0], []):
                    if ps:
                        if tok[2] == q and (q == "t" or wr or not k):
                            continue
                    elif not (k or wr) or not hit(r, x) or (q == "t" and tok[2] == q):
                        continue
                    need[tok[0]] = max(need.get(tok[0], 0), tok[1])
        for sem, val in sorted(need.items(), key=lambda z: (z[0][0] == "q", -z[1])):
            wait(q, sem, val)

    def note(q, reads, writes, tok):
        for wr, refs in ((False, reads), (True, writes)):
            for r in refs:
                old = acc.get(r[0], [])
                if wr:
                    old = [o for o in old if not (r[3] == 1 and r[1] <= o[0][1] and o[0][2] <= r[2] and (r[4] is None or r[4] == o[0][4]))]
                else:
                    old = [o for o in old if not (not o[1] and o[0] == r and o[2][2] == tok[2] and not tok[3] and not o[2][3])]
                acc[r[0]] = old + [(r, wr, tok)]

    def op(q, reads, writes, fns):
        deps(q, reads, writes, False)
        for f in fns[:-1]:
            f(Q[q])
        cnt[q] += 1
        sem = "q" + q
        fns[-1](Q[q]).then_inc(T.sem[sem], 1)
        top[sem] = cnt[q]
        s = dict(known[q]); s[sem] = cnt[q]
        snap[(sem, cnt[q])] = s
        note(q, reads, writes, (sem, cnt[q], q, False))

    def dma(q, out, in_, oap, iap):
        rd, wr = ([in_] if in_ else []), ([out] if out else [])
        deps(q, rd, wr, True)
        sem = "d%d" % nd[0]; nd[0] += 1
        Q[q].dma_start(out=oap, in_=iap).then_inc(T.sem[sem], 16)
        top[sem] = 16
        snap[(sem, 16)] = dict(known[q])
        note(q, rd, wr, (sem, 16, q, True))

    def remote(src, lsem, lval, call):
        deps("g", [src], [], True)
        call()
        top[lsem] = lval
        note("g", [src], [], (lsem, lval, "g", True))

    def land(refs, sem, val):
        top[sem] = val
        for r in refs:
            acc[r[0]] = [o for o in acc.get(r[0], []) if not hit(r, o[0])] + [(r, True, (sem, val, "-", True))]

    def finish():
        for sem, val in sorted(top.items()):
            wait("g", sem, val)
    return op, dma, remote, land, finish


def rank_program(g, core, T, topo):
    rank = T.rank_of(core)
    if rank is None:
        return
    op, dma, remote, land, finish = tracker(g, T)

    def R(n, a=0, b=None, step=1, row=None):
        if n in AL:
            o, w = AL[n]
            return ("pf", o + a, o + (w if b is None else b), step, row)
        return (n, a, (SCRATCH[n][1][1] if b is None else b), step, row)

    def ap(r):
        if r[4] is not None:
            return T[r[0]][r[4]::16, r[1]:r[2]]
        return T[r[0]][:, r[1]:r[2]] if r[3] == 1 else T[r[0]][:, r[1]:r[2]:r[3]]

    def ts(out, a, s1, o1, s2=None, o2=None):
        rd = [a] + [s for s in (s1, s2) if isinstance(s, tuple)]
        f1 = ap(s1) if isinstance(s1, tuple) else s1
        f2 = ap(s2) if isinstance(s2, tuple) else s2
        if o2 is None:
            op("v", rd, [out], [lambda e: e.tensor_scalar(out=ap(out), in0=ap(a), scalar1=f1, scalar2=None, op0=o1)])
        else:
            op("v", rd, [out], [lambda e: e.tensor_scalar(out=ap(out), in0=ap(a), scalar1=f1, scalar2=f2, op0=o1, op1=o2)])

    def tt(out, a, b, o):
        op("v", [a, b], [out], [lambda e: e.tensor_tensor(out=ap(out), in0=ap(a), in1=ap(b), op=o)])

    def cp(out, a):
        op("v", [a], [out], [lambda e: e.tensor_copy(out=ap(out), in_=ap(a))])

    def act(out, a, scale=1.0, bias=0.0):
        rd = [a] + ([scale] if isinstance(scale, tuple) else [])
        sc = ap(scale) if isinstance(scale, tuple) else scale
        op("s", rd, [out], [lambda e: e.activation(out=ap(out), in_=ap(a), func=CP, bias=bias, scale=sc)])

    def fill(r, c):
        op("v", [], [r], [lambda e: e.memset(ap(r), c)])

    def gat(q, out, win, off):
        if q == "v":
            op("v", [win, off], [out], [lambda e: e.tensor_copy(out=ap(out), in_=ap(win).indirect(ap(off)))])
        else:
            op("s", [win, off], [out], [lambda e: e.activation(out=ap(out), in_=ap(win).indirect(ap(off)), func=CP)])

    def gat2(out, win, off, b, o):
        op("v", [win, off, b], [out], [lambda e: e.tensor_tensor(out=ap(out), in0=ap(win).indirect(ap(off)), in1=ap(b), op=o)])

    def sca(win, off, a):
        op("v", [a, off], [win], [lambda e: e.tensor_copy(out=ap(win).indirect(ap(off)), in_=ap(a))])

    def f2p(ps, c0, z, src, a0, n):
        def mk(i):
            return lambda e: e.matmul(T[ps][:, c0:c0 + n], T[z][:, 128 * i:128 * i + 128], T[src][:, a0 + i:a0 + 16 * n:16], i == 0, i == 15)
        op("t", [R(z), R(src, a0, a0 + 16 * n)], [R(ps)], [mk(i) for i in range(16)])

    def p2f(tab, row, col, src, c0, n):
        out = R(tab, col, col + 16 * n, 1, row)
        dma("y", out, R(src, c0, c0 + n), ap(out), T[src][:, c0:c0 + n])

    def route(c):
        r = T.rank_of(c)
        nb = [T.cores[(r - 1) % NR], T.cores[(r + 1) % NR]]
        e = [topo.engines(c, d) for d in nb]
        first = 0 if len(e[0]) <= len(e[1]) else 1
        for k in (8, 4, 2, 1):
            x = e[first][:k]
            y = [z for z in e[1 - first] if z not in x][-k:]
            if len(x) == k and len(y) == k:
                return nb, ([x, y] if first == 0 else [y, x]), k

    nb, eng, kk = route(core)
    arrive = route(nb[0])[2] + route(nb[1])[2]

    def send(kind, t, src, dst, d0, w):
        tr = []
        for s in range(2):
            rid, pid, _se = topo.addr(nb[s])
            tr.append(RemoteDMATransfer(dst_ids=[DstId(rid=rid, pnc=pid)], dma_engine_mask=sum(1 << z for z in eng[s]),
                                        remote_sem=T.sem["a%s%d" % (kind, t)], src=T[src][:, s * w:s * w + w],
                                        dst=T[dst][:, d0 + (1 - s) * w:d0 + (2 - s) * w]))
        ls = "l%s%d" % (kind, t)
        remote(R(src), ls, 2 * kk, lambda: g.remote_dma_fused(tr, local_sem=T.sem[ls]))

    def arrived(kind, t, dst, d0, w):
        land([R(dst, d0, d0 + 2 * w)], "a%s%d" % (kind, t), arrive)

    def load(q, out, src):
        dma(q, out, None, ap(out), src)
    load("s", R("xin", 320, 480), T.bs[:, :])
    load("y", R("xin", 0, 160), T.lt[:, :])
    load("s", R("xin", 160, 320), T.rt[:, :])
    for s in range(2):
        load("y", R("sin", 8 * s, 8 * s + 8), T.snd[:, 128 * s:128 * s + 128])
    load("y", R("ev", 0, P0), T.err[:, :])
    load("y", R("win", 0, 1), T.wt[:, :])
    load("y", R("win", 1, 2), T.th[:, :])
    load("s", R("dr"), T.det[:, :])

    op("g", [], [R("pid", 0, 1)], [lambda e: e.iota(T.pid[:, 0:1], [[1, 1]], 0, 1)])

    def iof(n, a, b, pat, base):
        op("g", [], [R(n, a, b)], [lambda e: e.iota(T[n][:, a:b], pat, base, 0, allow_small_or_imprecise_dtypes=True)])
    fill(R("bo"), 1.0)
    iof("cc", 0, 224, [[1, 224]], 0)
    op("g", [R("bo")], [R("bo")], [lambda e: e.affine_select(T.bo[:, :], T.bo[:, :], [[-16, 8], [0, 16]], A.is_ge, 0.0, 0, 1)])
    op("g", [R("bo")], [R("bo")], [lambda e: e.affine_select(T.bo[:, :], T.bo[:, :], [[16, 8], [0, 16]], A.is_ge, 0.0, 15, -1)])
    iof("i16", 0, 16, [[1, 16]], 0)
    iof("ev", P0, 3600, [[0, 1040]], 0)
    iof("xs", 0, 16, [[128, 2], [1, 8]], GH)
    iof("gv", 0, 256, [[128, 2], [1, 16], [16, 8]], 16)
    op("g", [R("bo")], [R("ltm")], [lambda e: e.affine_select(T.ltm[:, :], T.bo[:, :], [[1, 128]], A.is_gt, 0.0, 0, -1)])
    ts(R("pid", 1, 2), R("pid", 0, 1), 15, A.bitwise_and)
    fill(R("zz"), 0.0)
    ts(R("pid", 2, 3), R("pid", 1, 2), 1, A.logical_shift_right)
    cp(R("ci", 0, 1), R("pid", 1, 2))
    cp(R("ci", 1, 2), R("pid", 2, 3))
    fill(R("tb"), 8192.0)
    I1 = R("ci", 0, 1)
    ts(R("ci", 6, 7), I1, float(W0), A.add)
    ts(R("mk2"), R("i16", 0, 8), R("ci", 1, 2), A.is_equal)
    ts(R("ix"), R("cc"), 16.0, A.mult, R("ci", 6, 7), A.add)

    def halves(src, a, b, h, l, ha, q="v"):
        if q == "s":
            act(R(h, ha, ha + b - a), R(src, a, b))
        else:
            cp(R(h, ha, ha + b - a), R(src, a, b))
        tt(R(l, ha, ha + b - a), R(src, a, b), R(h, ha, ha + b - a), A.subtract)
    OFF = {"l": 0, "r": 224, "b": 448}
    TROW = {"b": 0, "r": 2, "l": 6}

    def table(x, t, q="v"):
        o, n = OFF[x], 160 + 32 * t
        halves("px", o, o + n, "hi", "lo", o, q)
        for k, src in ((0, "hi"), (1, "lo")):
            for tab in (("tc", "tb") if t and x == "b" else ("tb",)):
                p2f(tab, TROW[x] + k, 0, src, o, 160)
                if t:
                    p2f(tab, TROW[x] + k, P0, src, o + 160, 32)

    def slots(t):
        halves("sn", 0, 16, "shi", "slo", 0)
        for k, src in ((0, "shi"), (1, "slo")):
            for s in range(2):
                p2f("snf", k, 128 * s, src, 8 * s, 8)

    def nat(s, i, src):
        a = 128 * s + 16 * (i & 7) + (i >> 3)
        return lambda e: e.matmul(T.ps0[:, 8 * s:8 * s + 8], T.zb[:, 128 * i:128 * i + 128], T[src][:, a:a + 15:2], i == 0, i == 15)

    def bases(src, tab):
        gat("s", R(src), R(tab), R("snu"))
        for s in range(2):
            op("t", [R("zb"), R(src)], [R("ps0")], [nat(s, i, src) for i in range(16)])

    def sendbases(t):
        cp(R("bes"), R("ps0", 0, 16))
        send("be", t, "bes", "bel%d" % t, 0, 8)

    halves("ix", 0, 224, "ihi", "ilo", 0)
    for k, src in ((4, "ihi"), (5, "ilo")):
        p2f("tb", k, 0, src, 0, 160)
        p2f("tb", k, P0, src, 160, 32)
    for x, c in (("b", 320), ("l", 0), ("r", 160)):
        cp(R("px", OFF[x], OFF[x] + 160), R("xin", c, c + 160))
        table(x, 0, "s")
    cp(R("sn"), R("sin"))
    cp(R("snu"), R("sn"))
    op("v", [R("bo")], [R("zz")], [lambda e, i=i: e.tensor_copy(out=T.zz[:, 129 * i:128 * i + 128:16], in_=T.bo[:, i::16]) for i in range(16)])
    ts(R("zb"), R("zz"), R("mk2", 0, 1), A.mult)
    fill(R("snf"), 0.0)
    slots(0)
    ts(R("bv", 0, 160), R("px", 448, 608), float(GH - 1), A.min)
    ts(R("ci", 2, 3), I1, 160.0, A.mult)
    ts(R("ci", 3, 4), I1, 32.0, A.mult, 2400.0, A.add)
    ts(R("ci", 4, 5), I1, 32.0, A.mult, 2880.0, A.add)
    ts(R("ci", 5, 6), I1, 8.0, A.mult)
    bases("gs", "tb")
    ts(R("me", 0, 160), R("cc", 0, 160), R("ci", 2, 3), A.add)
    ts(R("me", 160, 192), R("cc", 160, 192), R("ci", 3, 4), A.add)
    ts(R("me", 192, 224), R("cc", 192, 224), R("ci", 4, 5), A.add)
    ts(R("xs"), R("xs"), R("ci", 5, 6), A.add)
    ts(R("mk"), R("i16"), I1, A.is_equal)
    ts(R("i8", 1, 2), R("mk2", 0, 1), 4096.0, A.mult)
    ts(R("snf", 256, 272), R("i16"), 0.0, A.mult, R("i8", 1, 2), A.add)
    for w in ("eu", "wa", "wb"):
        fill(R(w, 0, 16), 0.0)
    sendbases(0)
    ts(R("zr"), R("zz"), R("mk2", 1, 2), A.mult)
    ts(R("zl"), R("zz"), R("mk2", 3, 4), A.mult)
    ts(R("zi"), R("zz"), R("mk2", 2, 3), A.mult)
    cp(R("gh1"), R("gv"))
    tt(R("gl1"), R("gv"), R("gh1"), A.subtract)
    ts(R("gh1"), R("gh1"), R("mk", 4, 5), A.mult)
    ts(R("gl1"), R("gl1"), R("mk", 5, 6), A.mult)
    tt(R("gi"), R("gh1"), R("gl1"), A.add)
    errors = [None]

    for t in range(2):
        n = 160 + 32 * t
        NL, base = 16 * n, P0 + 512 * t
        nw0 = n
        h = n // 2
        E = ((0, h), (h, n))
        NE = [(W0 + 16 * a, W0 + 16 * b) for a, b in E]
        EC = [R("ec", 16 * a, 16 * b) for a, b in E]
        ntb = "nt%d" % t
        PL, PR, PB = R("px", 0, n), R("px", 224, 224 + n), R("px", 448, 448 + n)
        ME, WIN = R("me", 0, n), R("tb")
        WE = R("eu", 0, W0 + NL)

        def keep(src, k):
            act(EC[k], R(src, *NE[k]))
        if t == 0:
            gat("s", R("x0"), R("ev", 0, 3600), R("snu"))
            send("x0", t, "x0", "eu", 16, 128)
        else:
            gat("s", R("gs"), WIN, R("snu"))
        f2p("ps1", 0, "zl", "gs", 0, 16)
        f2p("ps1", 16, "zr", "gs", 0, 16)
        f2p("ps1", 32, "zi", "gs", 0, 16)
        gat("s", R("gb", 0, NL), WIN, R("bv", 0, n))
        cp(R("slu"), R("ps1", 0, 32))
        ts(R("siu"), R("ps1", 32, 48), -float(W0), A.add)
        tt(R("srf"), R("ps1", 16, 32), R("xs"), A.is_equal)
        f2p("ps2", 0, "zb", "gb", 0, n)
        f2p("ps3", 0, "zi", "gb", 0, n)
        f2p("ps4", 0, "zr", "gb", 0, n)
        cp(R("lv", 0, n), PL)
        cp(R("rv", 0, n), PR)
        if t:
            errors[0]()
            gat("s", R("x0"), R("eu", W0, W0 + NL), R("siu"))
            send("x0", t, "x0", "eu", 16, 128)
            keep("eu", 0)
            keep("eu", 1)
        arrived("be", t, "bel%d" % t, 0, 8)
        bl = "bel%d" % t
        ts(R("gm"), R(bl), 3712.0, A.is_ge)
        ts(R("gm1"), R(bl, 8, 16), 3584.0, A.is_ge)
        ts(R("gd", 0, 8), R(bl, 0, 8), -3968.0, A.add)
        ts(R("gd", 8, 16), R(bl, 8, 16), -3712.0, A.add)
        tt(R("gm", 8, 16), R("gm1"), R("gm", 8, 16), A.subtract)
        tt(R("gd"), R("gd"), R("gm"), A.mult)
        ts(R("gbu"), R("gd"), 256.0, A.add)
        gat2(R("tb", GH, 3840), R("snf"), R("gbu"), R("gi"), A.add)
        for k, (a, b) in enumerate(E):
            gat("v", R("gl", 16 * a, 16 * b), WIN, R("lv", a, b))
            if k == 0:
                gat("s", R("gx"), WIN, R("slu"))
            gat("s", R("gr", 16 * a, 16 * b), WIN, R("rv", a, b))
        for k, (a, b) in enumerate(E):
            f2p("ps5" if k == 0 else "ps7", 0, "zb", "gl", 16 * a, b - a)
            f2p("ps6" if k == 0 else "ps0", 0, "zi", "gl", 16 * a, b - a)
            if k == 0:
                f2p("ps1", 0, "zb", "gx", 0, 32)
                f2p("ps1", 32, "zi", "gx", 0, 32)
        if t == 0:
            op("v", [R("ev", 0, P0)], [R("eu", W0, W0 + P0)],
               [lambda e, i=i: e.tensor_copy(out=T.eu[:, W0 + i:W0 + P0:16], in_=T.ev[:, 160 * i:160 * i + 160]) for i in range(16)])
            keep("eu", 0)
            keep("eu", 1)

        def legs(ps, ps2, a, b, v, f, w):
            tt(R(v, a, b), R(ps, 0, b - a), R("me", a, b), A.is_equal)
            tt(R(f, a, b), R(ps2, 0, b - a), R(v, a, b), A.mult)
            cp(R(w, a, b), R(f, a, b))
        legs("ps5", "ps6", E[0][0], E[0][1], "vl", "lf", "lw")
        for x in (0, 16):
            tt(R("xv", x, x + 16), R("ps1", x, x + 16), R("sn"), A.is_equal)
        tt(R("xf"), R("ps1", 32, 64), R("xv"), A.mult)
        cp(R("xlu"), R("xf"))
        arrived("x0", t, "eu", 16, 128)
        gat2(R("wa", *NE[0]), WE, R("lw", *E[0]), EC[0], A.max)
        gat2(R("x1"), WE, R("xlu", 0, 16), R("x0"), A.max)
        gat2(R("x1"), WE, R("xlu", 16, 32), R("x1"), A.max)
        send("x1", t, "x1", "wa", 16, 128)
        if t == 0:
            iof("cv", 0, 3072, [[0, 3072]], 1)
        legs("ps7", "ps0", E[1][0], E[1][1], "vl", "lf", "lw")
        gat2(R("wa", *NE[1]), WE, R("lw", *E[1]), EC[1], A.max)
        for k, (a, b) in enumerate(E):
            f2p("ps5" if k == 0 else "ps7", 0, "zb", "gr", 16 * a, b - a)
            f2p("ps6" if k == 0 else "ps0", 0, "zi", "gr", 16 * a, b - a)
            legs("ps5" if k == 0 else "ps7", "ps6" if k == 0 else "ps0", a, b, "vr", "rf", "rw")
            gat2(R("wa", *NE[k]), WE, R("rw", a, b), R("wa", *NE[k]), A.max)
            keep("wa", k)
        f2p("ps5", 0, "zr", "gl", 0, n)
        f2p("ps6", 0, "zr", "gr", 0, n)
        arrived("x1", t, "wa", 16, 128)
        WWA, WWB = R("wa", 0, W0 + NL), R("wb", 0, W0 + NL)
        gat2(R("x2"), WWA, R("xlu", 0, 16), R("x1"), A.max)
        gat2(R("x2"), WWA, R("xlu", 16, 32), R("x2"), A.max)
        send("x2", t, "x2", "wb", 16, 128)
        if t == 0:
            for tab in ("nt0", "tc", "nt1"):
                iof(tab, 0, 3840, [[0, 3840]], 0)
            act(R("df"), R("dr"), 0.5, -0.25)
            act(R("df"), R("df"), 1.0, 8388608.0)

        def bulk(dst, win):
            for k in range(2):
                gat2(R(dst, *NE[k]), win, R("lw", *E[k]), EC[k], A.max)
            for k in range(2):
                gat2(R(dst, *NE[k]), win, R("rw", *E[k]), R(dst, *NE[k]), A.max)
                keep(dst, k)
        bulk("wb", WWA)
        tt(R("eq", 0, n), R("ps2", 0, n), ME, A.is_equal)
        tt(R("pt", 0, n), PB, ME, A.is_gt)
        tt(R("bf", 0, n), R("ps3", 0, n), R("eq", 0, n), A.mult)
        tt(R("pt", 0, n), R("pt", 0, n), R("eq", 0, n), A.mult)
        cp(R("bw", 0, n), R("bf", 0, n))
        ts(R("thr", 0, n), R("pt", 0, n), -93.0, A.mult, 99.0, A.add)
        tt(R("rb", 0, n), R("ps4", 0, n), ME, A.is_equal)
        tt(R("rl", 0, n), R("ps5", 0, n), ME, A.is_equal)
        tt(R("rr", 0, n), R("ps6", 0, n), ME, A.is_equal)
        if t == 0:
            cp(R("ci", 7, 8), R("win", 1, 2))
            cp(R("i8", 0, 1), R("win", 0, 1))
            fill(R("zero"), 0.0)
            fill(R("dh", 2048, 2064), 0.0)
            ts(R("ixm"), R("ix", 0, 192), -16.0, A.add)
            halves("me", 0, 224, "chi", "clo", 0, "s")
            for k, src in ((0, "chi"), (1, "clo")):
                p2f("cv", k, 0, src, 0, 160)
                p2f("cv", k, P0, src, 160, 32)
            for k in range(3):
                act(R("px", 224 * k + 192, 224 * k + 224), R("me", 192, 224))
            act(R("dh", 0, 2048), R("df"), 1.0, -8388608.0)
            act(R("zh"), R("zz"), R("i8", 0, 1))
        TH = R("ci", 7, 8)
        fill(R("ct", 0, 256), 0.0)
        arrived("x2", t, "wb", 16, 128)
        bulk("wa", WWB)
        if t == 0:
            op("s", [R("cv")], [R("vf")],
               [lambda e, i=i: e.activation(out=T.vf[:, i:P0:16], in_=T.cv[:, 160 * i:160 * i + 160], func=CP) for i in range(16)] +
               [lambda e, i=i: e.activation(out=T.vf[:, P0 + i:3072:16], in_=T.cv[:, P0 + 32 * i:P0 + 32 * i + 32], func=CP) for i in range(16)])
        else:
            op("s", [R("eu", W0, W0 + 3072)], [R("ev", 0, 3072)],
               [lambda e, i=i: e.activation(out=T.ev[:, 160 * i:160 * i + 160], in_=T.eu[:, W0 + i:W0 + P0:16], func=CP) for i in range(16)] +
               [lambda e, i=i: e.activation(out=T.ev[:, P0 + 32 * i:P0 + 32 * i + 32], in_=T.eu[:, W0 + P0 + i:W0 + 3072:16], func=CP) for i in range(16)])
        for k, (a, b) in enumerate(E):
            gat2(R("hb", 16 * a, 16 * b), WWA, R("bw", a, b), EC[k], A.max)
            ts(R("hb", 16 * a, 16 * b), R("hb", 16 * a, 16 * b), TH, A.is_ge)
            f2p("ps4", a, "zz", "hb", 16 * a, b - a)
        tt(R("hot", 0, n), R("ps4", 0, n), R("thr", 0, n), A.is_ge)
        segs = [(0, 160)] + ([(160, 192)] if t else [])
        for a, b in segs:
            op("v", [R("hot", a, b), R("zero", a, b)], [R("cum", a, b)],
               [lambda e, a=a, b=b: e.tensor_tensor_scan(T.cum[:, a:b], T.hot[:, a:b], T.zero[:, a:b], 0.0, A.add, A.add)])
        op("t", [R("ltm"), R("cum", 0, 160)], [R("ps0")], [lambda e: e.matmul(T.ps0[:, 0:1], T.ltm[:, :], T.cum[:, 159:160], True, True)])
        if t:
            op("t", [R("ltm"), R("bo"), R("cum")], [R("ps0")],
               [lambda e: e.matmul(T.ps0[:, 1:2], T.ltm[:, :], T.cum[:, 191:192], True, False),
                lambda e: e.matmul(T.ps0[:, 1:2], T.bo[:, :], T.cum[:, 159:160], False, True)])
        for k, (a, b) in enumerate(segs):
            ts(R("k1", a, b), R("cum", a, b), R("ps0", k, k + 1), A.add)
        ts(R("sel", 0, n), R("k1", 0, n), 256.0, A.is_le)
        ts(R("kn", 0, n), R("k1", 0, n), 2.0, A.mult, -2.0, A.add)
        tt(R("sel", 0, n), R("sel", 0, n), R("hot", 0, n), A.mult)
        act(R("n1", 0, n), R("sel", 0, n), float(base))
        act(R("wr", 0, n), R("sel", 0, n), -BIG, BIG - 1.0)
        tt(R("n0", 0, n), R("kn", 0, n), R("sel", 0, n), A.mult)

        def rows(lst):
            for row, src in lst:
                p2f(ntb, row, 0, src, 0, 160)
                if t:
                    p2f(ntb, row, P0, src, 160, 32)
        rows(((1, "n1"), (0, "n0")))
        gat("s", R("gb", 0, NL), R(ntb), R("bv", 0, n))
        tt(R("dd", 0, n), R("wr", 0, n), R("k1", 0, n), A.add)
        tt(R("dd", 0, n), R("dd", 0, n), R("ixm", 0, n), A.min)
        cp(R("pd", 0, n), R("dd", 0, n))
        sp = 96 + 16 * t
        sca(R("ct", 0, 256 + NL), R("pd", 0, sp), R("vf", 0, 16 * sp))
        f2p("ps1", 0, "zz", "gb", 0, n)
        tt(R("nc", 0, n), R("ps1", 0, n), R("eq", 0, n), A.mult)
        ts(R("sc", 0, n), R("nc", 0, n), 1.0, A.min)
        halves("nc", 0, n, "nchi", "nclo", 0)
        rows(((4, "sc"), (2, "nchi"), (3, "nclo")))
        sca(R("ct", 0, 256 + NL), R("pd", sp, n), R("vf", 16 * sp, NL))

        def ctp(ps, c, z):
            op("t", [R(z), R("ct", 0, 256)], [R(ps)],
               [lambda e, i=i: e.matmul(T[ps][:, c:c + 16], T[z][:, 128 * i:128 * i + 128], T.ct[:, 16 * i:16 * i + 16], i == 0, i == 15) for i in range(16)])
        ctp("ps2", 0, "zr")
        ctp("ps2", 16, "zb")
        gat("s", R("gb", 0, NL), R(ntb), R("bv", 0, n))
        tt(R("nt", 0, n), R("n0", 0, n), R("n1", 0, n), A.add)
        tt(R("nc", 0, n), R("nc", 0, n), R("sc", 0, n), A.add)
        ts(R("st", 0, n), R("nt", 0, n), 1.0, A.min)
        tt(R("spl", 0, n), R("st", 0, n), R("sc", 0, n), A.add)
        for s in range(2):
            ts(R("fl", s, 32, 2), R("ps2", 0, 16), 0.5, A.mult)
        ts(R("fo"), R("fl"), -float(GH), A.mult, float(GH), A.add)
        tt(R("tv", 0, 32, 2), R("ps2", 16, 32), R("fo", 0, 32, 2), A.add)
        cp(R("tu16"), R("tv", 0, 32, 2))
        gat("s", R("gt"), WIN, R("tu16"))
        act(R("m8", 0, n), R("spl", 0, n), 8192.0)
        f2p("ps3", 0, "zb", "gt", 0, 16)
        f2p("ps0", 0, "zz", "gb", 0, n)
        tt(R("no", 0, n), R("nt", 0, n), R("nc", 0, n), A.add)
        tt(R("tv", 1, 32, 2), R("ps3", 0, 16), R("fl", 0, 32, 2), A.mult)
        tt(R("tv", 1, 32, 2), R("tv", 1, 32, 2), R("fo", 0, 32, 2), A.add)
        cp(R("tu"), R("tv"))
        gat("s", R("gq"), WIN, R("tu"))
        f2p("ps6", 0, "zr", "gq", 0, 32)
        if t == 0:
            f2p("ps6", 32, "zi", "gq", 0, 32)
        gat("v", R("gl", 0, 16 * h), R(ntb), R("lv", 0, h))
        cp(R("rq"), R("ps6", 0, 32))
        cp(R("yu"), R("rq"))
        gat("s", R("gy"), WIN, R("yu"))
        gat("s", R("gn"), R(ntb), R("yu"))
        gat("s", R("eg"), R("ev", 0, 3600), R("tu"))
        f2p("ps2", 0, "zr", "gy", 0, 32)
        f2p("ps3", 0, "zz", "gn", 0, 32)
        f2p("ps7", 0, "zh", "eg", 0, 32)
        if t == 0:
            gat("s", R("gsn"), R(ntb), R("snu"))
            f2p("ps1", 0, "zz", "gsn", 0, 16)
        tt(R("wq", 0, n), R("ps0", 0, n), R("rb", 0, n), A.mult)
        gat("v", R("gl", 16 * h, NL), R(ntb), R("lv", h, n))
        tt(PB, PB, R("wq", 0, n), A.max)
        tt(R("nb", 0, n), R("no", 0, n), R("st", 0, n), A.add)
        tt(PB, PB, R("m8", 0, n), A.subtract)
        tt(R("nb", 0, n), R("nb", 0, n), R("sc", 0, n), A.subtract)
        dump = 2800.0 if t == 0 else 3328.0

        def detlists():
            tt(R("di", 0, 32), R("ps7", 0, 32), R("tv"), A.add)
            tt(R("di", 32, 64), R("ps7", 0, 32), R("me", nw0, nw0 + 32), A.add)
            ts(R("da"), R("di"), 2047, A.bitwise_and)
            ts(R("dq"), R("da"), -2048.0, A.add)
            tt(R("dq", 32, 64), R("dq", 32, 64), R("fl"), A.mult)
            ts(R("du"), R("dq"), 2048.0, A.add)
            gat("s", R("dg"), R("dh"), R("du"))

        def places():
            if t == 0:
                ts(R("scf"), R("ps6", 32, 64), -(W0 + dump), A.add)
            else:
                ts(R("scf"), R("tv"), -dump, A.add)
            tt(R("scf"), R("scf"), R("ix", 0, 32), A.subtract)
            tt(R("scf"), R("scf"), R("fl"), A.mult)
            tt(R("scf"), R("scf"), R("ix", 0, 32), A.add)
            ts(R("scu"), R("scf"), dump, A.add)
            ts(R("e2"), R("eg"), 0.5, A.mult, -0.25, A.add)

        def children(t=t):
            tt(R("cl"), R("e2"), R("dg", 0, 512), A.add)
            if t == 0:
                sca(R("eu", W0, 3856), R("scu"), R("cl"))
                tt(R("eu", W0 + P0, W0 + 3072), R("e2"), R("dg", 512, 1024), A.add)
            else:
                sca(R("ev"), R("scu"), R("cl"))
                tt(R("cr"), R("e2"), R("dg", 512, 1024), A.add)
                op("v", [R("cr")], [R("ev", 3072, GH)],
                   [lambda e, i=i: e.tensor_copy(out=T.ev[:, 3072 + 32 * i:3104 + 32 * i], in_=T.cr[:, i::16]) for i in range(16)])
        if t == 1:
            detlists()
            places()
        gat("s", R("gr", 0, NL), R(ntb), R("rv", 0, n))
        f2p("ps4", 0, "zz", "gl", 0, n)
        f2p("ps5", 0, "zz", "gr", 0, n)
        MN = R("me", nw0, nw0 + 32)

        def newplaces(k, x):
            o = R("px", 224 * k + nw0, 224 * k + nw0 + 32)
            w = R("nw", 32 * k, 32 * k + 32)
            tt(w, R(x), MN, A.subtract)
            tt(w, w, R("fl"), A.mult)
            tt(o, w, MN, A.add)
        tt(R("rn"), R("ps2", 0, 32), R("tv"), A.is_equal)
        tt(R("rn"), R("ps3", 0, 32), R("rn"), A.mult)
        tt(R("rn"), R("rn"), R("rq"), A.max)
        newplaces(2, "rn")
        tt(R("wq", 0, n), R("ps4", 0, n), R("rl", 0, n), A.mult)
        tt(PL, PL, R("wq", 0, n), A.max)
        tt(R("wq", 0, n), PL, R("spl", 0, n), A.mult)
        tt(PB, PB, R("wq", 0, n), A.max)
        if t == 0:
            table("b", 1)
            tt(R("sw"), R("ps1", 0, 16), R("srf"), A.mult)
            tt(R("sn"), R("sn"), R("sw"), A.max)
            cp(R("snu"), R("sn"))
            bases("gsb", "tc")
        tt(PL, PL, R("m8", 0, n), A.subtract)
        cp(R("pv", 0, 32, 2), R("tv", 1, 32, 2))
        tt(PL, PL, R("no", 0, n), A.max)
        cp(R("pv", 1, 32, 2), R("tv", 0, 32, 2))
        newplaces(0, "pv")
        if t == 0:
            table("l", 1)
            slots(1)
        tt(PR, PR, R("m8", 0, n), A.subtract)
        newplaces(1, "tv")
        if t == 1:
            children()
            dma("y", None, R("ev", 0, GH), T.ye[:, :], T.ev[:, 0:GH])
        tt(R("wq", 0, n), R("ps5", 0, n), R("rr", 0, n), A.mult)
        tt(R("wq", 0, n), R("wq", 0, n), R("m8", 0, n), A.subtract)
        tt(PR, PR, R("wq", 0, n), A.max)
        tt(PR, PR, R("nb", 0, n), A.max)
        if t == 0:
            table("r", 1)
            sendbases(1)
            ts(R("bv"), R("px", 448, 640), float(GH - 1), A.min)
            detlists()
            places()
            errors[0] = children

    for k, y in ((2, T.yb), (0, T.yl), (1, T.yr)):
        for a, b, c in ((0, P0, 0), (P0, 3072, 160), (3072, GH, 192)):
            src = R("px", 224 * k + c, 224 * k + c + (b - a) // 16)
            dma("y", None, src, y[:, a:b], ap(src))
    finish()
